import numpy as np
import ml_dtypes


def mxq(x, axis, fmt="e4m3"):
    dtype, down = {"e4m3": (ml_dtypes.float8_e4m3fn, 7), "e5m2": (ml_dtypes.float8_e5m2, 14)}[fmt]
    v = np.moveaxis(np.asarray(x, np.float32).astype(ml_dtypes.bfloat16).astype(np.float64), axis, -1)
    blocks = v.reshape(v.shape[:-1] + (-1, 32))
    amax = np.abs(blocks).max(-1, keepdims=True)
    byte = np.maximum(np.where(amax > 0, np.frexp(amax)[1] - 1 + 127, 0) - down, 1)
    scale = np.exp2(byte - 127.0)
    codes = (blocks / scale).astype(np.float32).astype(dtype).astype(np.float64)
    return np.moveaxis((codes * scale).reshape(v.shape), -1, axis)


WIDE = False


def mx_kscale(k):
    if not WIDE:
        return np.ones(k)
    levels = np.array([10, -10, 5, -5, 0])
    if k % 512:
        return np.exp2(np.random.permutation(np.resize(levels, k // 32))).repeat(32)
    a = np.empty((k // 512, 16))
    for p in range(k // 512):
        a[p, :8] = np.random.permutation(np.resize(levels, 8))
        for g in range(8):
            far = levels[np.abs(levels - a[p, g]) >= 10]
            a[p, g + 8] = far[np.random.randint(len(far))]
    return np.exp2(a.ravel()).repeat(32)


def f64(x):
    return np.asarray(x).astype(np.float64)


def striped(idx):
    return np.tile(idx.reshape(-1, 16).T, (8, 1)).astype(np.uint16)


def unstriped(offs):
    return offs[:16].T.reshape(-1).astype(np.int64)


def striped8(idx):
    return np.concatenate([x.reshape(-1, 16).T for x in idx]).astype(np.uint16)


def runs(offs, k):
    lists = np.stack([offs[16 * r : 16 * r + 16].T.reshape(-1) for r in range(8)]).astype(np.int64)
    return lists[np.arange(k) % 512 // 64]


def pack_weight(w):
    k, n = w.shape
    w = f64(np.asarray(w, np.float32).astype(ml_dtypes.bfloat16)).reshape(k // 32, 32, n)
    amax = np.abs(w).max(1)
    byte = np.clip(np.where(amax > 0, np.frexp(amax)[1] - 1 + 127 - 7, 1), 1, 254)
    scaled = (w * np.exp2(127.0 - byte)[:, None, :]).reshape(k, n).astype(np.float32)
    words = np.ascontiguousarray(scaled.reshape(k // 512, 128, 4, n).transpose(0, 1, 3, 2)).astype(ml_dtypes.float8_e4m3fn).view(np.uint8)
    return words, np.ascontiguousarray(byte.astype(np.uint8).reshape(k // 512, 16, n))


def unpack_weight(words, scales):
    g, p, n, _ = words.shape
    vals = np.ascontiguousarray(words).view(ml_dtypes.float8_e4m3fn).astype(np.float64) * np.repeat(np.exp2(scales.astype(np.float64) - 127.0), 8, axis=1)[..., None]
    return vals.transpose(0, 1, 3, 2).reshape(g * 512, n)


def relu(v):
    return np.maximum(v, 0.0)


def sigmoid(v):
    return 1.0 / (1.0 + np.exp(-np.maximum(v, -700.0)))

def planes(y):
    n, m = y.shape
    v = y.astype(np.float32).astype(ml_dtypes.bfloat16).astype(np.float64).reshape(n // 32, 32, m)
    top = np.abs(v).max(1)
    byte = np.clip(np.where(top > 0, np.frexp(top)[1] - 1 + 127 - 7, 1), 1, 254)
    codes = (v * np.exp2(127.0 - byte)[:, None, :]).reshape(n, m).astype(np.float32).astype(ml_dtypes.float8_e4m3fn).view(np.uint8)
    words = codes.reshape(n // 512, 128, 4, m).transpose(0, 1, 3, 2)
    return np.ascontiguousarray(words), np.ascontiguousarray(byte.astype(np.uint8).reshape(n // 512, 16, m))


K, T, S, N, H = 512, 2048, 512, 512, 512


def setup_inputs():
    n = np.random.standard_normal
    s = mx_kscale(K)[:, None]
    u = mx_kscale(S)
    packed_xT = pack_weight(n((K, T)) * s)
    packed_w1 = pack_weight(n((S, N)) / np.sqrt(S) / u[:, None])
    return {
        "x_words": packed_xT[0],
        "x_scales": packed_xT[1],
        "wa": (n((K, H)) / np.sqrt(K) / s).astype(np.float32),
        "gt": (np.random.uniform(0.5, 1.5, (S, 1)) * u[:, None]).astype(np.float32),
        "w1_words": packed_w1[0],
        "w1_scales": packed_w1[1],
        "offs": striped(np.random.permutation(T)[:S]),
        "fo": striped8(np.stack([np.random.permutation(H) for _ in range(8)])),
    }


def reference(x_words, x_scales, wa, gt, w1_words, w1_scales, offs, fo):
    xq = unpack_weight(x_words, x_scales)[:, unstriped(offs)]
    y = xq.T @ mxq(f64(wa), 0, "e4m3")
    z = f64(gt) * relu(y)
    h = unpack_weight(w1_words, w1_scales).T @ mxq(z, 0, "e4m3")
    out_0 = h * (sigmoid(h[np.arange(N)[:, None], runs(fo, N)]))
    return (out_0,) + planes(out_0)

@@ -1,0 +1,197 @@
+from contextlib import ExitStack
+
+import concourse.mybir as mybir
+
+F32 = mybir.dt.float32
+BF16 = mybir.dt.bfloat16
+I32 = mybir.dt.int32
+U32 = mybir.dt.uint32
+U16 = mybir.dt.uint16
+U8 = mybir.dt.uint8
+FP8X4 = mybir.dt.float8_e4m3fn_x4
+ALU = mybir.AluOpType
+ACT = mybir.ActivationFunctionType
+
+P = 128
+PACK = 4
+T = 2048
+S = 512
+W = 128
+CHUNKS = S // W
+LIST_COLS = W // 16
+WA_LOADS = ((0, 2), (2, 4))
+FUSED = (3,)
+FLOPS = 2 * 2 * 512 * 512 * 512
+
+
+def tile_picked_mixpick_none_po_kernel(tc, x_words, x_scales, wa, gt, w1_words, w1_scales, offs, fo, out_0, out_1, out_2):
+    nc = tc.nc
+    with ExitStack() as ctx:
+        sb = ctx.enter_context(tc.tile_pool(name="sb", bufs=1))
+        ps = ctx.enter_context(tc.psum_pool(name="ps", bufs=1))
+
+        def tile(shape, dtype, name, tag=""):
+            return sb.tile(shape, dtype, name=name, tag=tag, align_bytes=64)
+
+        offs_t = sb.tile([P, S // 16], U16, name="offs_t")
+        fo_t = sb.tile([P, S // 16], U16, name="fo_t")
+        xs_win = tile([P, T], U8, "xs_win", "slot_a")
+        xw_win = tile([P, T], I32, "xw_win")
+        gt_t = tile([P, PACK], F32, "gt_t")
+        warm = tile([P, 1], F32, "warm", "slot_b")
+        warm_out = tile([P, 1], F32, "warm_out", "slot_d")
+
+        nc.gpsimd.memset(xs_win[:].bitcast(I32), 0)
+        nc.gpsimd.memset(warm[:], 0.0)
+
+        nc.sync.dma_start(offs_t[:], offs)
+        for q in range(4):
+            nc.scalar.dma_start(xs_win[32 * q : 32 * q + 4, :].bitcast(I32), x_scales[0, 4 * q : 4 * q + 4, :].bitcast(I32))
+        nc.sync.dma_start(xw_win[:], x_words[0].rearrange("p n t -> p (n t)").bitcast(I32))
+        nc.sync.dma_start(fo_t[:], fo)
+        nc.gpsimd.dma_start(gt_t[:], gt.rearrange("(p t) o -> p (t o)", t=PACK))
+        nc.scalar.activation(warm_out[:], warm[:], ACT.Sigmoid)
+        wa_rows = wa.rearrange("(p j) n -> p j n", j=PACK)
+        wa_raw = {}
+        for a, b in WA_LOADS:
+            raw = tile([P, PACK, (b - a) * W], F32, f"wa_raw{a}", "slot_b" if a else "")
+            nc.sync.dma_start(raw[:], wa_rows[:, :, a * W : b * W])
+            for c in range(a, b):
+                wa_raw[c] = raw[:, :, (c - a) * W : (c - a + 1) * W]
+
+        xs_got = tile([P, S], U8, "xs_got", "slot_c")
+        xs = tile([P, S], U8, "xs")
+        xw = tile([P, S], U32, "xw", "slot_c")
+        nc.vector.tensor_copy(xs_got[:], xs_win[:].indirect(offs_t[:]))
+        nc.vector.tensor_copy(xs[:].rearrange("p (t m) -> p t m", t=PACK), xs_got[:].rearrange("p (m t) -> p t m", t=PACK))
+        nc.vector.tensor_copy(xw[:].rearrange("p (t m) -> p m t", t=PACK), xw_win[:].bitcast(U32).indirect(offs_t[:]))
+
+        w1w_raw = tile([P, S], I32, "w1w_raw", "slot_d")
+        nc.sync.dma_start(w1w_raw[:], w1_words[0].rearrange("p n t -> p (n t)").bitcast(I32))
+        w1s_raw = tile([P, S], U8, "w1s_raw", "slot_a")
+        nc.gpsimd.memset(w1s_raw[:].bitcast(I32), 0)
+        for q in range(4):
+            nc.sync.dma_start(w1s_raw[32 * q : 32 * q + 4, :].bitcast(I32), w1_scales[0, 4 * q : 4 * q + 4, :].bitcast(I32))
+        w1s = tile([P, S], U8, "w1s")
+        w1w = tile([P, S], I32, "w1w")
+
+        def interleaved(dst, src):
+            return (
+                dst.rearrange("p (c i t) -> p c t i", i=4, t=PACK),
+                src.rearrange("p t (c i) -> p c t i", i=4),
+            )
+
+        wa_q, wa_s, z_q, z_s, y_ps, h_ps, z_bf = {}, {}, {}, {}, {}, {}, {}
+        h_win = [tile([P, S], F32, f"h_win{t}") for t in range(PACK)]
+        sig_win = {t: tile([P, S], F32, f"sig_win{t}") for t in FUSED}
+
+        def wa_stage(c):
+            bf = tile([P, W * PACK], BF16, f"wa_bf{c}")
+            dst, src = interleaved(bf[:], wa_raw[c])
+            if c == 0:
+                nc.vector.tensor_copy(dst, src)
+            else:
+                nc.scalar.copy(dst, src)
+            wa_q[c] = tile([P, W], U32, f"wa_q{c}")
+            wa_s[c] = tile([P, W], U8, f"wa_s{c}")
+            nc.vector.quantize_mx(wa_q[c][:].bitcast(FP8X4), wa_s[c][:], bf[:])
+
+        def product(bank, lhs_w, lhs_s, rhs_w, rhs_s):
+            for t in range(PACK):
+                cols = slice(t * P, (t + 1) * P)
+                nc.tensor.matmul_mx(
+                    out=bank[:, t, :],
+                    lhsT=lhs_w[:, cols].bitcast(FP8X4),
+                    lhsT_scale=lhs_s[:, cols],
+                    rhs=rhs_w[:].bitcast(FP8X4),
+                    rhs_scale=rhs_s[:],
+                    start=True,
+                    stop=True,
+                )
+
+        def y_stage(c):
+            y_ps[c] = ps.tile([P, PACK, W], F32, name=f"y_ps{c}")
+            product(y_ps[c], xw, xs, wa_q[c], wa_s[c])
+            z_bf[c] = tile([P, W, PACK], BF16, f"z_bf{c}")
+            nc.vector.scalar_tensor_tensor(
+                out=z_bf[c][:],
+                in0=y_ps[c][:].rearrange("p t j -> p j t"),
+                scalar=0.0,
+                in1=gt_t[:].unsqueeze(1).to_broadcast([P, W, PACK]),
+                op0=ALU.max,
+                op1=ALU.mult,
+            )
+
+        def h_stage(c):
+            z_q[c] = tile([P, W], U32, f"z_q{c}")
+            z_s[c] = tile([P, W], U8, f"z_s{c}")
+            nc.vector.quantize_mx(z_q[c][:].bitcast(FP8X4), z_s[c][:], z_bf[c][:].rearrange("p j t -> p (j t)"))
+            h_ps[c] = ps.tile([P, PACK, W], F32, name=f"h_ps{c}")
+            product(h_ps[c], w1w, w1s, z_q[c], z_s[c])
+            cols = slice(c * W, (c + 1) * W)
+            for t in range(PACK):
+                if t in FUSED:
+                    nc.scalar.activation(sig_win[t][:, cols], h_ps[c][:, t, :], ACT.Sigmoid)
+                if c == CHUNKS - 1 and t > 0:
+                    nc.vector.tensor_copy(h_win[t][:, cols], h_ps[c][:, t, :])
+                else:
+                    nc.scalar.copy(h_win[t][:, cols], h_ps[c][:, t, :])
+
+        wa_stage(0)
+        wa_stage(1)
+        y_stage(0)
+        y_stage(1)
+        wa_stage(2)
+        wa_stage(3)
+        nc.vector.tensor_copy(w1w[:].rearrange("p (t m) -> p t m", t=PACK), w1w_raw[:].rearrange("p (m t) -> p t m", t=PACK))
+        nc.vector.tensor_copy(w1s[:].rearrange("p (t m) -> p t m", t=PACK), w1s_raw[:].rearrange("p (m t) -> p t m", t=PACK))
+        h_stage(0)
+        y_stage(2)
+        h_stage(1)
+        y_stage(3)
+        h_stage(2)
+        h_stage(3)
+
+        out_rows = out_0.rearrange("(p t) j -> p t j", t=PACK)
+        out_words = out_1[0].rearrange("p n t -> p (n t)").bitcast(I32)
+        o_s = tile([P, S], U8, "o_s")
+        o_q = [tile([P, S - W], I32, "o_q_head"), tile([P, W], I32, "o_q_tail")]
+        o32, o_bf = {}, {}
+        plain = [t for t in range(PACK) if t not in FUSED]
+
+        def gate_stage(c):
+            cols = slice(c * W, (c + 1) * W)
+            picks = fo_t[:, c * LIST_COLS : (c + 1) * LIST_COLS]
+            sig = tile([P, len(plain), W], F32, f"sig{c}")
+            o32[c] = tile([P, PACK, W], F32, f"o32_{c}")
+            for t in plain:
+                nc.scalar.activation(sig[:, t, :], h_win[t][:].indirect(picks), ACT.Sigmoid)
+            for t in FUSED:
+                nc.vector.tensor_tensor(o32[c][:, t, :], sig_win[t][:].indirect(picks), h_win[t][:, cols], ALU.mult)
+            nc.vector.tensor_tensor(o32[c][:, 0 : len(plain), :], h_ps[c][:, 0 : len(plain), :], sig[:], ALU.mult)
+            nc.sync.dma_start(out_rows[:, :, cols], o32[c][:])
+
+        def cast_stage(c):
+            o_bf[c] = tile([P, W * PACK], BF16, f"o_bf{c}")
+            dst, src = interleaved(o_bf[c][:], o32[c][:])
+            nc.vector.tensor_copy(dst, src)
+
+        def plane_stage(c):
+            cols = slice(c * W, (c + 1) * W)
+            codes = o_q[1][:] if c == CHUNKS - 1 else o_q[0][:, cols]
+            nc.vector.quantize_mx(codes.bitcast(FP8X4), o_s[:, cols], o_bf[c][:])
+            if c == CHUNKS - 2:
+                nc.sync.dma_start(out_words[:, 0 : S - W], o_q[0][:])
+            if c == CHUNKS - 1:
+                nc.sync.dma_start(out_words[:, S - W : S], o_q[1][:])
+
+        for c in range(CHUNKS + 2):
+            if c < CHUNKS:
+                gate_stage(c)
+            if 1 <= c <= CHUNKS:
+                cast_stage(c - 1)
+            if c >= 2:
+                plane_stage(c - 2)
+        for q in range(4):
+            eng = nc.scalar if q % 2 else nc.sync
+            eng.dma_start(out_2[0, 4 * q : 4 * q + 4, :].bitcast(I32), o_s[32 * q : 32 * q + 4, :].bitcast(I32))

@@ -18,9 +18,9 @@ T = 2048
 S = 512
 W = 128
 CHUNKS = S // W
+LAST = CHUNKS - 1
 LIST_COLS = W // 16
-WA_LOADS = ((0, 2), (2, 4))
-FUSED = (3,)
+ON_VECTOR = ((3,), (3,), (2, 3), (2, 3))
 FLOPS = 2 * 2 * 512 * 512 * 512
 
 
@@ -33,47 +33,8 @@ def tile_picked_mixpick_none_po_kernel(tc, x_words, x_scales, wa, gt, w1_words, 
         def tile(shape, dtype, name, tag=""):
             return sb.tile(shape, dtype, name=name, tag=tag, align_bytes=64)
 
-        offs_t = sb.tile([P, S // 16], U16, name="offs_t")
-        fo_t = sb.tile([P, S // 16], U16, name="fo_t")
-        xs_win = tile([P, T], U8, "xs_win", "slot_a")
-        xw_win = tile([P, T], I32, "xw_win")
-        gt_t = tile([P, PACK], F32, "gt_t")
-        warm = tile([P, 1], F32, "warm", "slot_b")
-        warm_out = tile([P, 1], F32, "warm_out", "slot_d")
-
-        nc.gpsimd.memset(xs_win[:].bitcast(I32), 0)
-        nc.gpsimd.memset(warm[:], 0.0)
-
-        nc.sync.dma_start(offs_t[:], offs)
-        for q in range(4):
-            nc.scalar.dma_start(xs_win[32 * q : 32 * q + 4, :].bitcast(I32), x_scales[0, 4 * q : 4 * q + 4, :].bitcast(I32))
-        nc.sync.dma_start(xw_win[:], x_words[0].rearrange("p n t -> p (n t)").bitcast(I32))
-        nc.sync.dma_start(fo_t[:], fo)
-        nc.gpsimd.dma_start(gt_t[:], gt.rearrange("(p t) o -> p (t o)", t=PACK))
-        nc.scalar.activation(warm_out[:], warm[:], ACT.Sigmoid)
-        wa_rows = wa.rearrange("(p j) n -> p j n", j=PACK)
-        wa_raw = {}
-        for a, b in WA_LOADS:
-            raw = tile([P, PACK, (b - a) * W], F32, f"wa_raw{a}", "slot_b" if a else "")
-            nc.sync.dma_start(raw[:], wa_rows[:, :, a * W : b * W])
-            for c in range(a, b):
-                wa_raw[c] = raw[:, :, (c - a) * W : (c - a + 1) * W]
-
-        xs_got = tile([P, S], U8, "xs_got", "slot_c")
-        xs = tile([P, S], U8, "xs")
-        xw = tile([P, S], U32, "xw", "slot_c")
-        nc.vector.tensor_copy(xs_got[:], xs_win[:].indirect(offs_t[:]))
-        nc.vector.tensor_copy(xs[:].rearrange("p (t m) -> p t m", t=PACK), xs_got[:].rearrange("p (m t) -> p t m", t=PACK))
-        nc.vector.tensor_copy(xw[:].rearrange("p (t m) -> p m t", t=PACK), xw_win[:].bitcast(U32).indirect(offs_t[:]))
-
-        w1w_raw = tile([P, S], I32, "w1w_raw", "slot_d")
-        nc.sync.dma_start(w1w_raw[:], w1_words[0].rearrange("p n t -> p (n t)").bitcast(I32))
-        w1s_raw = tile([P, S], U8, "w1s_raw", "slot_a")
-        nc.gpsimd.memset(w1s_raw[:].bitcast(I32), 0)
-        for q in range(4):
-            nc.sync.dma_start(w1s_raw[32 * q : 32 * q + 4, :].bitcast(I32), w1_scales[0, 4 * q : 4 * q + 4, :].bitcast(I32))
-        w1s = tile([P, S], U8, "w1s")
-        w1w = tile([P, S], I32, "w1w")
+        def dealt(eng, dst, src):
+            eng.tensor_copy(dst.rearrange("p (t m) -> p t m", t=PACK), src.rearrange("p (m t) -> p t m", t=PACK))
 
         def interleaved(dst, src):
             return (
@@ -81,37 +42,82 @@ def tile_picked_mixpick_none_po_kernel(tc, x_words, x_scales, wa, gt, w1_words, 
                 src.rearrange("p t (c i) -> p c t i", i=4),
             )
 
-        wa_q, wa_s, z_q, z_s, y_ps, h_ps, z_bf = {}, {}, {}, {}, {}, {}, {}
-        h_win = [tile([P, S], F32, f"h_win{t}") for t in range(PACK)]
-        sig_win = {t: tile([P, S], F32, f"sig_win{t}") for t in FUSED}
+        offs_t = sb.tile([P, S // 16], U16, name="offs_t")
+        fo_t = sb.tile([P, S // 16], U16, name="fo_t")
+        xs_win = tile([P, T], U8, "xs_win", "slot_a")
+        gt_t = tile([P, PACK], F32, "gt_t")
+        warm = tile([P, 1], F32, "warm")
+        warm_out = tile([P, 1], F32, "warm_out")
+        wa_raw = tile([P, PACK, S], F32, "wa_raw")
 
-        def wa_stage(c):
-            bf = tile([P, W * PACK], BF16, f"wa_bf{c}")
-            dst, src = interleaved(bf[:], wa_raw[c])
-            if c == 0:
-                nc.vector.tensor_copy(dst, src)
-            else:
-                nc.scalar.copy(dst, src)
-            wa_q[c] = tile([P, W], U32, f"wa_q{c}")
-            wa_s[c] = tile([P, W], U8, f"wa_s{c}")
-            nc.vector.quantize_mx(wa_q[c][:].bitcast(FP8X4), wa_s[c][:], bf[:])
+        w1s_raw = tile([P, S], U8, "w1s_raw")
+        nc.gpsimd.memset(xs_win[:].bitcast(I32), 0)
+        nc.gpsimd.memset(w1s_raw[:].bitcast(I32), 0)
+        nc.vector.memset(warm[:], 0.0)
+        for q in range(4):
+            nc.gpsimd.dma_start(w1s_raw[32 * q : 32 * q + 4, :].bitcast(I32), w1_scales[0, 4 * q : 4 * q + 4, :].bitcast(I32))
+        nc.scalar.activation(warm_out[:], warm[:], ACT.Sigmoid)
 
-        def product(bank, lhs_w, lhs_s, rhs_w, rhs_s):
-            for t in range(PACK):
+        nc.sync.dma_start(wa_raw[:], wa.rearrange("(p j) n -> p j n", j=PACK))
+        nc.sync.dma_start(offs_t[:], offs)
+        nc.sync.dma_start(fo_t[:], fo)
+        for q in range(4):
+            nc.sync.dma_start(xs_win[32 * q : 32 * q + 4, :].bitcast(I32), x_scales[0, 4 * q : 4 * q + 4, :].bitcast(I32))
+        xw_win = tile([P, T], I32, "xw_win", "slot_b")
+        nc.sync.dma_start(xw_win[:], x_words[0].rearrange("p n t -> p (n t)").bitcast(I32))
+        nc.sync.dma_start(gt_t[:], gt.rearrange("(p t) o -> p (t o)", t=PACK))
+        w1w_raw = tile([P, S], I32, "w1w_raw")
+        nc.sync.dma_start(w1w_raw[:], w1_words[0].rearrange("p n t -> p (n t)").bitcast(I32))
+
+        wa_bf, wa_q, wa_s, z_q, z_s, y_ps, h_ps, z_bf = {}, {}, {}, {}, {}, {}, {}, {}
+        for half in range(2):
+            wa_bf[half] = tile([P, 2 * W * PACK], BF16, f"wa_bf{half}")
+            dst, src = interleaved(wa_bf[half][:], wa_raw[:, :, 2 * half * W : 2 * (half + 1) * W])
+            nc.scalar.copy(dst, src)
+
+        def wa_quant(half, tag):
+            codes = tile([P, 2 * W], U32, f"wa_q{half}", tag)
+            scales = tile([P, 2 * W], U8, f"wa_s{half}")
+            nc.vector.quantize_mx(codes[:].bitcast(FP8X4), scales[:], wa_bf[half][:])
+            for k in range(2):
+                wa_q[2 * half + k] = codes[:, k * W : (k + 1) * W]
+                wa_s[2 * half + k] = scales[:, k * W : (k + 1) * W]
+
+        xs_got = tile([P, S], U8, "xs_got", "slot_c")
+        xs = tile([P, S], U8, "xs")
+        nc.vector.tensor_copy(xs_got[:], xs_win[:].indirect(offs_t[:]))
+        dealt(nc.vector, xs[:], xs_got[:])
+        wa_quant(0, "slot_a")
+        xw = tile([P, S], U32, "xw", "slot_c")
+        nc.vector.tensor_copy(xw[:].rearrange("p (t m) -> p m t", t=PACK), xw_win[:].bitcast(U32).indirect(offs_t[:]))
+        wa_quant(1, "slot_b")
+
+        w1s = tile([P, S], U8, "w1s")
+        w1w = tile([P, S], I32, "w1w")
+        dealt(nc.gpsimd, w1s[:], w1s_raw[:])
+        dealt(nc.gpsimd, w1w[:], w1w_raw[:])
+
+        sig_tiles = sorted({t for c in range(CHUNKS) for t in ON_VECTOR[c]}, reverse=True)
+        raw_tiles = sorted({t for c in range(CHUNKS) for t in range(PACK) if t not in ON_VECTOR[c]})
+        h_win = {t: tile([P, S], F32, f"h_win{t}") for t in raw_tiles}
+        sig_win = {t: tile([P, S], F32, f"sig_win{t}") for t in sig_tiles}
+
+        def product(outs, lhs_w, lhs_s, rhs_w, rhs_s):
+            for t, out in outs:
                 cols = slice(t * P, (t + 1) * P)
                 nc.tensor.matmul_mx(
-                    out=bank[:, t, :],
+                    out=out,
                     lhsT=lhs_w[:, cols].bitcast(FP8X4),
                     lhsT_scale=lhs_s[:, cols],
-                    rhs=rhs_w[:].bitcast(FP8X4),
-                    rhs_scale=rhs_s[:],
+                    rhs=rhs_w.bitcast(FP8X4),
+                    rhs_scale=rhs_s,
                     start=True,
                     stop=True,
                 )
 
         def y_stage(c):
-            y_ps[c] = ps.tile([P, PACK, W], F32, name=f"y_ps{c}")
-            product(y_ps[c], xw, xs, wa_q[c], wa_s[c])
+            y_ps[c] = ps.tile([P, PACK, W], F32, name=f"y_ps{c}", tag=f"y{c}")
+            product([(t, y_ps[c][:, t, :]) for t in range(PACK)], xw, xs, wa_q[c], wa_s[c])
             z_bf[c] = tile([P, W, PACK], BF16, f"z_bf{c}")
             nc.vector.scalar_tensor_tensor(
                 out=z_bf[c][:],
@@ -126,25 +132,28 @@ def tile_picked_mixpick_none_po_kernel(tc, x_words, x_scales, wa, gt, w1_words, 
             z_q[c] = tile([P, W], U32, f"z_q{c}")
             z_s[c] = tile([P, W], U8, f"z_s{c}")
             nc.vector.quantize_mx(z_q[c][:].bitcast(FP8X4), z_s[c][:], z_bf[c][:].rearrange("p j t -> p (j t)"))
-            h_ps[c] = ps.tile([P, PACK, W], F32, name=f"h_ps{c}")
-            product(h_ps[c], w1w, w1s, z_q[c], z_s[c])
+            if c < LAST:
+                bank = ps.tile([P, PACK, W], F32, name=f"h_ps{c}")
+                h_ps[c] = [(0, PACK, bank)]
+            else:
+                h_ps[c] = [
+                    (2, PACK, ps.tile([P, 2, W], F32, name="h_ps_hi")),
+                    (0, 2, ps.tile([P, 2, W], F32, name="h_ps_lo", tag="y0")),
+                ]
+            where = {t: bank[:, t - a, :] for a, b, bank in h_ps[c] for t in range(a, b)}
+            order = [3, 2, 0, 1] if c == LAST else range(PACK)
+            product([(t, where[t]) for t in order], w1w, w1s, z_q[c][:], z_s[c][:])
             cols = slice(c * W, (c + 1) * W)
-            for t in range(PACK):
-                if t in FUSED:
-                    nc.scalar.activation(sig_win[t][:, cols], h_ps[c][:, t, :], ACT.Sigmoid)
-                if c == CHUNKS - 1 and t > 0:
-                    nc.vector.tensor_copy(h_win[t][:, cols], h_ps[c][:, t, :])
+            for t in sig_tiles:
+                nc.scalar.activation(sig_win[t][:, cols], where[t], ACT.Sigmoid)
+            for t in raw_tiles:
+                if c == LAST and t < 2:
+                    nc.vector.tensor_copy(h_win[t][:, cols], where[t])
                 else:
-                    nc.scalar.copy(h_win[t][:, cols], h_ps[c][:, t, :])
+                    nc.scalar.copy(h_win[t][:, cols], where[t])
 
-        wa_stage(0)
-        wa_stage(1)
         y_stage(0)
         y_stage(1)
-        wa_stage(2)
-        wa_stage(3)
-        nc.vector.tensor_copy(w1w[:].rearrange("p (t m) -> p t m", t=PACK), w1w_raw[:].rearrange("p (m t) -> p t m", t=PACK))
-        nc.vector.tensor_copy(w1s[:].rearrange("p (t m) -> p t m", t=PACK), w1s_raw[:].rearrange("p (m t) -> p t m", t=PACK))
         h_stage(0)
         y_stage(2)
         h_stage(1)
@@ -155,43 +164,48 @@ def tile_picked_mixpick_none_po_kernel(tc, x_words, x_scales, wa, gt, w1_words, 
         out_rows = out_0.rearrange("(p t) j -> p t j", t=PACK)
         out_words = out_1[0].rearrange("p n t -> p (n t)").bitcast(I32)
         o_s = tile([P, S], U8, "o_s")
-        o_q = [tile([P, S - W], I32, "o_q_head"), tile([P, W], I32, "o_q_tail")]
-        o32, o_bf = {}, {}
-        plain = [t for t in range(PACK) if t not in FUSED]
+        o_q = [tile([P, 2 * W], I32, f"o_q{half}") for half in range(2)]
+        o32, o_bf, sig = {}, {}, {}
+
+        for c in range(CHUNKS):
+            picks = fo_t[:, c * LIST_COLS : (c + 1) * LIST_COLS]
+            sig[c] = tile([P, PACK, W], F32, f"sig{c}")
+            for t in range(PACK):
+                if t in ON_VECTOR[c]:
+                    nc.vector.tensor_copy(sig[c][:, t, :], sig_win[t][:].indirect(picks))
+                else:
+                    nc.scalar.activation(sig[c][:, t, :], h_win[t][:].indirect(picks), ACT.Sigmoid)
 
         def gate_stage(c):
-            cols = slice(c * W, (c + 1) * W)
-            picks = fo_t[:, c * LIST_COLS : (c + 1) * LIST_COLS]
-            sig = tile([P, len(plain), W], F32, f"sig{c}")
             o32[c] = tile([P, PACK, W], F32, f"o32_{c}")
-            for t in plain:
-                nc.scalar.activation(sig[:, t, :], h_win[t][:].indirect(picks), ACT.Sigmoid)
-            for t in FUSED:
-                nc.vector.tensor_tensor(o32[c][:, t, :], sig_win[t][:].indirect(picks), h_win[t][:, cols], ALU.mult)
-            nc.vector.tensor_tensor(o32[c][:, 0 : len(plain), :], h_ps[c][:, 0 : len(plain), :], sig[:], ALU.mult)
-            nc.sync.dma_start(out_rows[:, :, cols], o32[c][:])
+            for a, b, bank in h_ps[c]:
+                nc.vector.tensor_tensor(o32[c][:, a:b, :], bank[:], sig[c][:, a:b, :], ALU.mult)
+            nc.sync.dma_start(out_rows[:, :, c * W : (c + 1) * W], o32[c][:])
 
-        def cast_stage(c):
+        def cast_stage(c, copy):
             o_bf[c] = tile([P, W * PACK], BF16, f"o_bf{c}")
             dst, src = interleaved(o_bf[c][:], o32[c][:])
-            nc.vector.tensor_copy(dst, src)
+            copy(dst, src)
 
         def plane_stage(c):
             cols = slice(c * W, (c + 1) * W)
-            codes = o_q[1][:] if c == CHUNKS - 1 else o_q[0][:, cols]
+            codes = o_q[c // 2][:, (c % 2) * W : (c % 2 + 1) * W]
             nc.vector.quantize_mx(codes.bitcast(FP8X4), o_s[:, cols], o_bf[c][:])
-            if c == CHUNKS - 2:
-                nc.sync.dma_start(out_words[:, 0 : S - W], o_q[0][:])
-            if c == CHUNKS - 1:
-                nc.sync.dma_start(out_words[:, S - W : S], o_q[1][:])
 
-        for c in range(CHUNKS + 2):
-            if c < CHUNKS:
-                gate_stage(c)
-            if 1 <= c <= CHUNKS:
-                cast_stage(c - 1)
-            if c >= 2:
-                plane_stage(c - 2)
+        gate_stage(0)
+        cast_stage(0, nc.vector.tensor_copy)
+        gate_stage(1)
+        cast_stage(1, nc.scalar.copy)
+        plane_stage(0)
+        gate_stage(2)
+        cast_stage(2, nc.scalar.copy)
+        gate_stage(3)
+        cast_stage(3, nc.vector.tensor_copy)
+        plane_stage(1)
+        nc.sync.dma_start(out_words[:, 0 : 2 * W], o_q[0][:])
+        plane_stage(3)
+        plane_stage(2)
+        nc.sync.dma_start(out_words[:, 2 * W : S], o_q[1][:])
         for q in range(4):
             eng = nc.scalar if q % 2 else nc.sync
             eng.dma_start(out_2[0, 4 * q : 4 * q + 4, :].bitcast(I32), o_s[32 * q : 32 * q + 4, :].bitcast(I32))

@@ -33,8 +33,11 @@ def tile_picked_mixpick_none_po_kernel(tc, x_words, x_scales, wa, gt, w1_words, 
         def tile(shape, dtype, name, tag=""):
             return sb.tile(shape, dtype, name=name, tag=tag, align_bytes=64)
 
-        def dealt(eng, dst, src):
-            eng.tensor_copy(dst.rearrange("p (t m) -> p t m", t=PACK), src.rearrange("p (m t) -> p t m", t=PACK))
+        def dealt(dst, src, run):
+            nc.vector.tensor_copy(
+                dst.rearrange("p (t c i) -> p c t i", t=PACK, i=run),
+                src.rearrange("p (c i t) -> p c t i", t=PACK, i=run),
+            )
 
         def interleaved(dst, src):
             return (
@@ -48,54 +51,61 @@ def tile_picked_mixpick_none_po_kernel(tc, x_words, x_scales, wa, gt, w1_words, 
         gt_t = tile([P, PACK], F32, "gt_t")
         warm = tile([P, 1], F32, "warm")
         warm_out = tile([P, 1], F32, "warm_out")
-        wa_raw = tile([P, PACK, S], F32, "wa_raw")
 
-        w1s_raw = tile([P, S], U8, "w1s_raw")
+        w1s_raw = tile([P, S], U8, "w1s_raw", "slot_e")
         nc.gpsimd.memset(xs_win[:].bitcast(I32), 0)
+        nc.gpsimd.memset(warm[:], 0.0)
         nc.gpsimd.memset(w1s_raw[:].bitcast(I32), 0)
-        nc.vector.memset(warm[:], 0.0)
         for q in range(4):
             nc.gpsimd.dma_start(w1s_raw[32 * q : 32 * q + 4, :].bitcast(I32), w1_scales[0, 4 * q : 4 * q + 4, :].bitcast(I32))
-        nc.scalar.activation(warm_out[:], warm[:], ACT.Sigmoid)
 
-        nc.sync.dma_start(wa_raw[:], wa.rearrange("(p j) n -> p j n", j=PACK))
+        wa_rows = wa.rearrange("(p j) n -> p j n", j=PACK)
+        wa_raw = {}
+
+        def wa_load(a, b):
+            raw = tile([P, PACK, (b - a) * W], F32, f"wa_raw{a}")
+            nc.sync.dma_start(raw[:], wa_rows[:, :, a * W : b * W])
+            for c in range(a, b):
+                wa_raw[c] = raw[:, :, (c - a) * W : (c - a + 1) * W]
+
         nc.sync.dma_start(offs_t[:], offs)
-        nc.sync.dma_start(fo_t[:], fo)
+        wa_load(0, 2)
         for q in range(4):
-            nc.sync.dma_start(xs_win[32 * q : 32 * q + 4, :].bitcast(I32), x_scales[0, 4 * q : 4 * q + 4, :].bitcast(I32))
+            (nc.scalar if q // 2 else nc.sync).dma_start(xs_win[32 * q : 32 * q + 4, :].bitcast(I32), x_scales[0, 4 * q : 4 * q + 4, :].bitcast(I32))
+        nc.scalar.activation(warm_out[:], warm[:], ACT.Sigmoid)
         xw_win = tile([P, T], I32, "xw_win", "slot_b")
         nc.sync.dma_start(xw_win[:], x_words[0].rearrange("p n t -> p (n t)").bitcast(I32))
-        nc.sync.dma_start(gt_t[:], gt.rearrange("(p t) o -> p (t o)", t=PACK))
-        w1w_raw = tile([P, S], I32, "w1w_raw")
+        wa_load(2, 4)
+        w1w_raw = tile([P, S], I32, "w1w_raw", "slot_d")
         nc.sync.dma_start(w1w_raw[:], w1_words[0].rearrange("p n t -> p (n t)").bitcast(I32))
+        nc.sync.dma_start(gt_t[:], gt.rearrange("(p t) o -> p (t o)", t=PACK))
+        nc.sync.dma_start(fo_t[:], fo)
 
         wa_bf, wa_q, wa_s, z_q, z_s, y_ps, h_ps, z_bf = {}, {}, {}, {}, {}, {}, {}, {}
-        for half in range(2):
-            wa_bf[half] = tile([P, 2 * W * PACK], BF16, f"wa_bf{half}")
-            dst, src = interleaved(wa_bf[half][:], wa_raw[:, :, 2 * half * W : 2 * (half + 1) * W])
+        for c in range(CHUNKS):
+            wa_bf[c] = tile([P, W * PACK], BF16, f"wa_bf{c}", f"bf{c}")
+            dst, src = interleaved(wa_bf[c][:], wa_raw[c])
             nc.scalar.copy(dst, src)
 
-        def wa_quant(half, tag):
-            codes = tile([P, 2 * W], U32, f"wa_q{half}", tag)
-            scales = tile([P, 2 * W], U8, f"wa_s{half}")
-            nc.vector.quantize_mx(codes[:].bitcast(FP8X4), scales[:], wa_bf[half][:])
-            for k in range(2):
-                wa_q[2 * half + k] = codes[:, k * W : (k + 1) * W]
-                wa_s[2 * half + k] = scales[:, k * W : (k + 1) * W]
+        def wa_quant(c, tag="", scale_tag=""):
+            codes = tile([P, W], U32, f"wa_q{c}", tag)
+            scales = tile([P, W], U8, f"wa_s{c}", scale_tag)
+            nc.vector.quantize_mx(codes[:].bitcast(FP8X4), scales[:], wa_bf[c][:])
+            wa_q[c], wa_s[c] = codes[:], scales[:]
 
         xs_got = tile([P, S], U8, "xs_got", "slot_c")
         xs = tile([P, S], U8, "xs")
         nc.vector.tensor_copy(xs_got[:], xs_win[:].indirect(offs_t[:]))
-        dealt(nc.vector, xs[:], xs_got[:])
+        dealt(xs[:], xs_got[:], 16)
         wa_quant(0, "slot_a")
+        wa_quant(1)
         xw = tile([P, S], U32, "xw", "slot_c")
         nc.vector.tensor_copy(xw[:].rearrange("p (t m) -> p m t", t=PACK), xw_win[:].bitcast(U32).indirect(offs_t[:]))
-        wa_quant(1, "slot_b")
 
-        w1s = tile([P, S], U8, "w1s")
+        w1s = tile([P, S], U8, "w1s", "slot_b")
         w1w = tile([P, S], I32, "w1w")
-        dealt(nc.gpsimd, w1s[:], w1s_raw[:])
-        dealt(nc.gpsimd, w1w[:], w1w_raw[:])
+        dealt(w1s[:], w1s_raw[:], 16)
+        dealt(w1w[:], w1w_raw[:], 4)
 
         sig_tiles = sorted({t for c in range(CHUNKS) for t in ON_VECTOR[c]}, reverse=True)
         raw_tiles = sorted({t for c in range(CHUNKS) for t in range(PACK) if t not in ON_VECTOR[c]})
@@ -118,7 +128,7 @@ def tile_picked_mixpick_none_po_kernel(tc, x_words, x_scales, wa, gt, w1_words, 
         def y_stage(c):
             y_ps[c] = ps.tile([P, PACK, W], F32, name=f"y_ps{c}", tag=f"y{c}")
             product([(t, y_ps[c][:, t, :]) for t in range(PACK)], xw, xs, wa_q[c], wa_s[c])
-            z_bf[c] = tile([P, W, PACK], BF16, f"z_bf{c}")
+            z_bf[c] = tile([P, W, PACK], BF16, f"z_bf{c}", f"bf{(c + 2) % CHUNKS}")
             nc.vector.scalar_tensor_tensor(
                 out=z_bf[c][:],
                 in0=y_ps[c][:].rearrange("p t j -> p j t"),
@@ -152,7 +162,9 @@ def tile_picked_mixpick_none_po_kernel(tc, x_words, x_scales, wa, gt, w1_words, 
                 else:
                     nc.scalar.copy(h_win[t][:, cols], where[t])
 
+        wa_quant(2, "slot_d")
         y_stage(0)
+        wa_quant(3)
         y_stage(1)
         h_stage(0)
         y_stage(2)

@@ -20,7 +20,7 @@ W = 128
 CHUNKS = S // W
 LAST = CHUNKS - 1
 LIST_COLS = W // 16
-ON_VECTOR = ((3,), (3,), (2, 3), (2, 3))
+ON_VECTOR = ((2, 3), (2, 3), (2, 3), (2, 3))
 FLOPS = 2 * 2 * 512 * 512 * 512
 
 
@@ -56,7 +56,7 @@ def tile_picked_mixpick_none_po_kernel(tc, x_words, x_scales, wa, gt, w1_words, 
         nc.gpsimd.memset(xs_win[:].bitcast(I32), 0)
         nc.gpsimd.memset(warm[:], 0.0)
         nc.gpsimd.memset(w1s_raw[:].bitcast(I32), 0)
-        for q in range(4):
+        for q in range(2):
             nc.gpsimd.dma_start(w1s_raw[32 * q : 32 * q + 4, :].bitcast(I32), w1_scales[0, 4 * q : 4 * q + 4, :].bitcast(I32))
 
         wa_rows = wa.rearrange("(p j) n -> p j n", j=PACK)
@@ -75,10 +75,12 @@ def tile_picked_mixpick_none_po_kernel(tc, x_words, x_scales, wa, gt, w1_words, 
         nc.scalar.activation(warm_out[:], warm[:], ACT.Sigmoid)
         xw_win = tile([P, T], I32, "xw_win", "slot_b")
         nc.sync.dma_start(xw_win[:], x_words[0].rearrange("p n t -> p (n t)").bitcast(I32))
+        for q in range(2, 4):
+            nc.sync.dma_start(w1s_raw[32 * q : 32 * q + 4, :].bitcast(I32), w1_scales[0, 4 * q : 4 * q + 4, :].bitcast(I32))
+        nc.sync.dma_start(gt_t[:], gt.rearrange("(p t) o -> p (t o)", t=PACK))
         wa_load(2, 4)
         w1w_raw = tile([P, S], I32, "w1w_raw", "slot_d")
         nc.sync.dma_start(w1w_raw[:], w1_words[0].rearrange("p n t -> p (n t)").bitcast(I32))
-        nc.sync.dma_start(gt_t[:], gt.rearrange("(p t) o -> p (t o)", t=PACK))
         nc.sync.dma_start(fo_t[:], fo)
 
         wa_bf, wa_q, wa_s, z_q, z_s, y_ps, h_ps, z_bf = {}, {}, {}, {}, {}, {}, {}, {}
@@ -176,12 +178,11 @@ def tile_picked_mixpick_none_po_kernel(tc, x_words, x_scales, wa, gt, w1_words, 
         out_rows = out_0.rearrange("(p t) j -> p t j", t=PACK)
         out_words = out_1[0].rearrange("p n t -> p (n t)").bitcast(I32)
         o_s = tile([P, S], U8, "o_s")
-        o_q = [tile([P, 2 * W], I32, f"o_q{half}") for half in range(2)]
         o32, o_bf, sig = {}, {}, {}
 
         for c in range(CHUNKS):
             picks = fo_t[:, c * LIST_COLS : (c + 1) * LIST_COLS]
-            sig[c] = tile([P, PACK, W], F32, f"sig{c}")
+            sig[c] = tile([P, PACK, W], F32, f"sig{c}", f"sig{c}")
             for t in range(PACK):
                 if t in ON_VECTOR[c]:
                     nc.vector.tensor_copy(sig[c][:, t, :], sig_win[t][:].indirect(picks))
@@ -205,18 +206,19 @@ def tile_picked_mixpick_none_po_kernel(tc, x_words, x_scales, wa, gt, w1_words, 
             nc.vector.quantize_mx(codes.bitcast(FP8X4), o_s[:, cols], o_bf[c][:])
 
         gate_stage(0)
-        cast_stage(0, nc.vector.tensor_copy)
+        cast_stage(0, nc.scalar.copy)
         gate_stage(1)
         cast_stage(1, nc.scalar.copy)
-        plane_stage(0)
         gate_stage(2)
         cast_stage(2, nc.scalar.copy)
         gate_stage(3)
+        o_q = [tile([P, 2 * W], I32, "o_q0", "sig3"), tile([P, 2 * W], I32, "o_q1")]
+        plane_stage(0)
         cast_stage(3, nc.vector.tensor_copy)
         plane_stage(1)
         nc.sync.dma_start(out_words[:, 0 : 2 * W], o_q[0][:])
-        plane_stage(3)
         plane_stage(2)
+        plane_stage(3)
         nc.sync.dma_start(out_words[:, 2 * W : S], o_q[1][:])
         for q in range(4):
             eng = nc.scalar if q % 2 else nc.sync

@@ -14,17 +14,22 @@ ACT = mybir.ActivationFunctionType
 
 P = 128
 PACK = 4
+QUADRANTS = 4
 T = 2048
 S = 512
 W = 128
 CHUNKS = S // W
 LAST = CHUNKS - 1
 LIST_COLS = W // 16
-ON_VECTOR = ((2, 3), (2, 3), (2, 3), (2, 3))
-FLOPS = 2 * 2 * 512 * 512 * 512
+LINE_BYTES = 16
+SCALAR_ROWS = (0, 1)
+VECTOR_ROWS = (3, 2)
+FLOPS = 2 * 2 * S * S * S
 
 
-def tile_picked_mixpick_none_po_kernel(tc, x_words, x_scales, wa, gt, w1_words, w1_scales, offs, fo, out_0, out_1, out_2):
+def tile_picked_mixpick_none_po_kernel(
+    tc, x_words, x_scales, wa, gt, w1_words, w1_scales, offs, fo, out_0, out_1, out_2
+):
     nc = tc.nc
     with ExitStack() as ctx:
         sb = ctx.enter_context(tc.tile_pool(name="sb", bufs=1))
@@ -33,107 +38,114 @@ def tile_picked_mixpick_none_po_kernel(tc, x_words, x_scales, wa, gt, w1_words, 
         def tile(shape, dtype, name, tag=""):
             return sb.tile(shape, dtype, name=name, tag=tag, align_bytes=64)
 
-        def dealt(dst, src, run):
-            nc.vector.tensor_copy(
+        def words_of(packed):
+            return packed[0].rearrange("p n t -> p (n t)").bitcast(I32)
+
+        def scale_rows(plane, rows, q):
+            return plane[32 * q : 32 * q + 4, :].bitcast(I32), rows[0, 4 * q : 4 * q + 4, :].bitcast(I32)
+
+        def deal(eng, dst, src, element_bytes):
+            run = LINE_BYTES // element_bytes
+            eng.tensor_copy(
                 dst.rearrange("p (t c i) -> p c t i", t=PACK, i=run),
                 src.rearrange("p (c i t) -> p c t i", t=PACK, i=run),
             )
 
         def interleaved(dst, src):
+            run = LINE_BYTES // 4
             return (
-                dst.rearrange("p (c i t) -> p c t i", i=4, t=PACK),
-                src.rearrange("p t (c i) -> p c t i", i=4),
+                dst.rearrange("p (c i t) -> p c t i", i=run, t=PACK),
+                src.rearrange("p t (c i) -> p c t i", i=run),
             )
 
         offs_t = sb.tile([P, S // 16], U16, name="offs_t")
         fo_t = sb.tile([P, S // 16], U16, name="fo_t")
-        xs_win = tile([P, T], U8, "xs_win", "slot_a")
+        xs_win = tile([P, T], U8, "xs_win", "after_byte_gather")
         gt_t = tile([P, PACK], F32, "gt_t")
         warm = tile([P, 1], F32, "warm")
         warm_out = tile([P, 1], F32, "warm_out")
+        w1s_raw = tile([P, S], U8, "w1s_raw")
 
-        w1s_raw = tile([P, S], U8, "w1s_raw", "slot_e")
         nc.gpsimd.memset(xs_win[:].bitcast(I32), 0)
         nc.gpsimd.memset(warm[:], 0.0)
         nc.gpsimd.memset(w1s_raw[:].bitcast(I32), 0)
-        for q in range(2):
-            nc.gpsimd.dma_start(w1s_raw[32 * q : 32 * q + 4, :].bitcast(I32), w1_scales[0, 4 * q : 4 * q + 4, :].bitcast(I32))
+        for q in range(QUADRANTS // 2):
+            nc.gpsimd.dma_start(*scale_rows(w1s_raw, w1_scales, q))
 
         wa_rows = wa.rearrange("(p j) n -> p j n", j=PACK)
         wa_raw = {}
 
-        def wa_load(a, b):
-            raw = tile([P, PACK, (b - a) * W], F32, f"wa_raw{a}")
-            nc.sync.dma_start(raw[:], wa_rows[:, :, a * W : b * W])
-            for c in range(a, b):
-                wa_raw[c] = raw[:, :, (c - a) * W : (c - a + 1) * W]
+        def load_wa_half(half):
+            raw = tile([P, PACK, 2 * W], F32, f"wa_raw{half}", f"after_wa_half{half}")
+            nc.sync.dma_start(raw[:], wa_rows[:, :, 2 * half * W : 2 * (half + 1) * W])
+            wa_raw[2 * half], wa_raw[2 * half + 1] = raw[:, :, 0:W], raw[:, :, W : 2 * W]
 
         nc.sync.dma_start(offs_t[:], offs)
-        wa_load(0, 2)
-        for q in range(4):
-            (nc.scalar if q // 2 else nc.sync).dma_start(xs_win[32 * q : 32 * q + 4, :].bitcast(I32), x_scales[0, 4 * q : 4 * q + 4, :].bitcast(I32))
+        load_wa_half(0)
+        for q in range(QUADRANTS):
+            queue = nc.sync if q < QUADRANTS // 2 else nc.scalar
+            queue.dma_start(*scale_rows(xs_win, x_scales, q))
         nc.scalar.activation(warm_out[:], warm[:], ACT.Sigmoid)
-        xw_win = tile([P, T], I32, "xw_win", "slot_b")
-        nc.sync.dma_start(xw_win[:], x_words[0].rearrange("p n t -> p (n t)").bitcast(I32))
-        for q in range(2, 4):
-            nc.sync.dma_start(w1s_raw[32 * q : 32 * q + 4, :].bitcast(I32), w1_scales[0, 4 * q : 4 * q + 4, :].bitcast(I32))
+        xw_win = tile([P, T], I32, "xw_win", "after_word_gather")
+        nc.sync.dma_start(xw_win[:], words_of(x_words))
+        load_wa_half(1)
         nc.sync.dma_start(gt_t[:], gt.rearrange("(p t) o -> p (t o)", t=PACK))
-        wa_load(2, 4)
-        w1w_raw = tile([P, S], I32, "w1w_raw", "slot_d")
-        nc.sync.dma_start(w1w_raw[:], w1_words[0].rearrange("p n t -> p (n t)").bitcast(I32))
+        for q in range(QUADRANTS // 2, QUADRANTS):
+            nc.sync.dma_start(*scale_rows(w1s_raw, w1_scales, q))
+        w1w_raw = tile([P, S], I32, "w1w_raw")
+        nc.sync.dma_start(w1w_raw[:], words_of(w1_words))
         nc.sync.dma_start(fo_t[:], fo)
 
-        wa_bf, wa_q, wa_s, z_q, z_s, y_ps, h_ps, z_bf = {}, {}, {}, {}, {}, {}, {}, {}
-        for c in range(CHUNKS):
-            wa_bf[c] = tile([P, W * PACK], BF16, f"wa_bf{c}", f"bf{c}")
-            dst, src = interleaved(wa_bf[c][:], wa_raw[c])
-            nc.scalar.copy(dst, src)
+        wa_bf = [tile([P, W * PACK], BF16, f"wa_bf{c}", f"after_wa_quant{c}") for c in range(CHUNKS)]
+        for c in range(LAST):
+            nc.scalar.copy(*interleaved(wa_bf[c][:], wa_raw[c]))
 
-        def wa_quant(c, tag="", scale_tag=""):
-            codes = tile([P, W], U32, f"wa_q{c}", tag)
-            scales = tile([P, W], U8, f"wa_s{c}", scale_tag)
-            nc.vector.quantize_mx(codes[:].bitcast(FP8X4), scales[:], wa_bf[c][:])
-            wa_q[c], wa_s[c] = codes[:], scales[:]
+        def quantised(values, name, tag=""):
+            codes = tile([P, W], U32, f"{name}_q", tag)
+            scales = tile([P, W], U8, f"{name}_s")
+            nc.vector.quantize_mx(codes[:].bitcast(FP8X4), scales[:], values)
+            return codes[:], scales[:]
 
-        xs_got = tile([P, S], U8, "xs_got", "slot_c")
+        xs_got = tile([P, S], U8, "xs_got", "after_byte_deal")
         xs = tile([P, S], U8, "xs")
         nc.vector.tensor_copy(xs_got[:], xs_win[:].indirect(offs_t[:]))
-        dealt(xs[:], xs_got[:], 16)
-        wa_quant(0, "slot_a")
-        wa_quant(1)
-        xw = tile([P, S], U32, "xw", "slot_c")
+        deal(nc.vector, xs[:], xs_got[:], 1)
+        wa_mx = {0: quantised(wa_bf[0][:], "wa0", "after_byte_gather"), 1: quantised(wa_bf[1][:], "wa1")}
+        xw = tile([P, S], U32, "xw", "after_byte_deal")
         nc.vector.tensor_copy(xw[:].rearrange("p (t m) -> p m t", t=PACK), xw_win[:].bitcast(U32).indirect(offs_t[:]))
 
-        w1s = tile([P, S], U8, "w1s", "slot_b")
-        w1w = tile([P, S], I32, "w1w")
-        dealt(w1s[:], w1s_raw[:], 16)
-        dealt(w1w[:], w1w_raw[:], 4)
+        w1s = tile([P, S], U8, "w1s", "after_word_gather")
+        deal(nc.vector, w1s[:], w1s_raw[:], 1)
+        nc.vector.tensor_copy(*interleaved(wa_bf[LAST][:], wa_raw[LAST]))
+        wa_mx[3] = quantised(wa_bf[3][:], "wa3")
+        wa_mx[2] = quantised(wa_bf[2][:], "wa2")
+        w1w = tile([P, S], I32, "w1w", "after_wa_quant3")
+        deal(nc.gpsimd, w1w[:], w1w_raw[:], 4)
 
-        sig_tiles = sorted({t for c in range(CHUNKS) for t in ON_VECTOR[c]}, reverse=True)
-        raw_tiles = sorted({t for c in range(CHUNKS) for t in range(PACK) if t not in ON_VECTOR[c]})
-        h_win = {t: tile([P, S], F32, f"h_win{t}") for t in raw_tiles}
-        sig_win = {t: tile([P, S], F32, f"sig_win{t}") for t in sig_tiles}
+        h_win = {t: tile([P, S], F32, f"h_win{t}") for t in SCALAR_ROWS}
+        sig_win = {t: tile([P, S], F32, f"sig_win{t}") for t in VECTOR_ROWS}
+        z_bf, h_banks = {}, {}
 
-        def product(outs, lhs_w, lhs_s, rhs_w, rhs_s):
-            for t, out in outs:
+        def product(outs, lhs_words, lhs_scales, rhs):
+            for t, out in outs.items():
                 cols = slice(t * P, (t + 1) * P)
                 nc.tensor.matmul_mx(
                     out=out,
-                    lhsT=lhs_w[:, cols].bitcast(FP8X4),
-                    lhsT_scale=lhs_s[:, cols],
-                    rhs=rhs_w.bitcast(FP8X4),
-                    rhs_scale=rhs_s,
+                    lhsT=lhs_words[:, cols].bitcast(FP8X4),
+                    lhsT_scale=lhs_scales[:, cols],
+                    rhs=rhs[0].bitcast(FP8X4),
+                    rhs_scale=rhs[1],
                     start=True,
                     stop=True,
                 )
 
-        def y_stage(c):
-            y_ps[c] = ps.tile([P, PACK, W], F32, name=f"y_ps{c}", tag=f"y{c}")
-            product([(t, y_ps[c][:, t, :]) for t in range(PACK)], xw, xs, wa_q[c], wa_s[c])
-            z_bf[c] = tile([P, W, PACK], BF16, f"z_bf{c}", f"bf{(c + 2) % CHUNKS}")
+        def z_stage(c, tag=""):
+            bank = ps.tile([P, PACK, W], F32, name=f"y_ps{c}", tag=f"y{c}")
+            product({t: bank[:, t, :] for t in range(PACK)}, xw, xs, wa_mx[c])
+            z_bf[c] = tile([P, W, PACK], BF16, f"z_bf{c}", tag)
             nc.vector.scalar_tensor_tensor(
                 out=z_bf[c][:],
-                in0=y_ps[c][:].rearrange("p t j -> p j t"),
+                in0=bank[:].rearrange("p t j -> p j t"),
                 scalar=0.0,
                 in1=gt_t[:].unsqueeze(1).to_broadcast([P, W, PACK]),
                 op0=ALU.max,
@@ -141,85 +153,80 @@ def tile_picked_mixpick_none_po_kernel(tc, x_words, x_scales, wa, gt, w1_words, 
             )
 
         def h_stage(c):
-            z_q[c] = tile([P, W], U32, f"z_q{c}")
-            z_s[c] = tile([P, W], U8, f"z_s{c}")
-            nc.vector.quantize_mx(z_q[c][:].bitcast(FP8X4), z_s[c][:], z_bf[c][:].rearrange("p j t -> p (j t)"))
-            if c < LAST:
-                bank = ps.tile([P, PACK, W], F32, name=f"h_ps{c}")
-                h_ps[c] = [(0, PACK, bank)]
-            else:
-                h_ps[c] = [
-                    (2, PACK, ps.tile([P, 2, W], F32, name="h_ps_hi")),
-                    (0, 2, ps.tile([P, 2, W], F32, name="h_ps_lo", tag="y0")),
-                ]
-            where = {t: bank[:, t - a, :] for a, b, bank in h_ps[c] for t in range(a, b)}
-            order = [3, 2, 0, 1] if c == LAST else range(PACK)
-            product([(t, where[t]) for t in order], w1w, w1s, z_q[c][:], z_s[c][:])
+            z_mx = quantised(z_bf[c][:].rearrange("p j t -> p (j t)"), f"z{c}")
             cols = slice(c * W, (c + 1) * W)
-            for t in sig_tiles:
-                nc.scalar.activation(sig_win[t][:, cols], where[t], ACT.Sigmoid)
-            for t in raw_tiles:
-                if c == LAST and t < 2:
-                    nc.vector.tensor_copy(h_win[t][:, cols], where[t])
-                else:
-                    nc.scalar.copy(h_win[t][:, cols], where[t])
+            if c < LAST:
+                h_banks[c] = [(0, PACK, ps.tile([P, PACK, W], F32, name=f"h_ps{c}"))]
+                rows, copy = range(PACK), nc.scalar.copy
+            else:
+                h_banks[c] = [
+                    (2, PACK, ps.tile([P, 2, W], F32, name="h_ps_upper")),
+                    (0, 2, ps.tile([P, 2, W], F32, name="h_ps_lower", tag="y0")),
+                ]
+                rows, copy = VECTOR_ROWS + SCALAR_ROWS, nc.vector.tensor_copy
+            h = {t: bank[:, t - a, :] for a, b, bank in h_banks[c] for t in range(a, b)}
+            product({t: h[t] for t in rows}, w1w, w1s, z_mx)
+            for t in VECTOR_ROWS:
+                nc.scalar.activation(sig_win[t][:, cols], h[t], ACT.Sigmoid)
+            for t in SCALAR_ROWS:
+                copy(h_win[t][:, cols], h[t])
 
-        wa_quant(2, "slot_d")
-        y_stage(0)
-        wa_quant(3)
-        y_stage(1)
+        z_stage(0, "after_wa_half1")
+        z_stage(1, "after_wa_quant2")
         h_stage(0)
-        y_stage(2)
+        z_stage(2)
         h_stage(1)
-        y_stage(3)
+        z_stage(3)
         h_stage(2)
         h_stage(3)
 
         out_rows = out_0.rearrange("(p t) j -> p t j", t=PACK)
-        out_words = out_1[0].rearrange("p n t -> p (n t)").bitcast(I32)
-        o_s = tile([P, S], U8, "o_s")
-        o32, o_bf, sig = {}, {}, {}
+        out_scales = tile([P, S], U8, "out_scales")
+        gate, out_f32, out_bf = {}, {}, {}
 
-        for c in range(CHUNKS):
+        def fetch_stage(c):
             picks = fo_t[:, c * LIST_COLS : (c + 1) * LIST_COLS]
-            sig[c] = tile([P, PACK, W], F32, f"sig{c}", f"sig{c}")
-            for t in range(PACK):
-                if t in ON_VECTOR[c]:
-                    nc.vector.tensor_copy(sig[c][:, t, :], sig_win[t][:].indirect(picks))
-                else:
-                    nc.scalar.activation(sig[c][:, t, :], h_win[t][:].indirect(picks), ACT.Sigmoid)
+            gate[c] = tile([P, PACK, W], F32, f"gate{c}", f"gate_slot{c % 2}")
+            for t in SCALAR_ROWS:
+                nc.scalar.activation(gate[c][:, t, :], h_win[t][:].indirect(picks), ACT.Sigmoid)
+            for t in sorted(VECTOR_ROWS):
+                nc.vector.tensor_copy(gate[c][:, t, :], sig_win[t][:].indirect(picks))
 
         def gate_stage(c):
-            o32[c] = tile([P, PACK, W], F32, f"o32_{c}")
-            for a, b, bank in h_ps[c]:
-                nc.vector.tensor_tensor(o32[c][:, a:b, :], bank[:], sig[c][:, a:b, :], ALU.mult)
-            nc.sync.dma_start(out_rows[:, :, c * W : (c + 1) * W], o32[c][:])
+            out_f32[c] = tile([P, PACK, W], F32, f"out_f32_{c}")
+            for a, b, bank in h_banks[c]:
+                nc.vector.tensor_tensor(out_f32[c][:, a:b, :], bank[:], gate[c][:, a:b, :], ALU.mult)
+            nc.sync.dma_start(out_rows[:, :, c * W : (c + 1) * W], out_f32[c][:])
 
-        def cast_stage(c, copy):
-            o_bf[c] = tile([P, W * PACK], BF16, f"o_bf{c}")
-            dst, src = interleaved(o_bf[c][:], o32[c][:])
-            copy(dst, src)
+        def round_stage(c, copy):
+            out_bf[c] = tile([P, W * PACK], BF16, f"out_bf{c}")
+            copy(*interleaved(out_bf[c][:], out_f32[c][:]))
 
-        def plane_stage(c):
-            cols = slice(c * W, (c + 1) * W)
-            codes = o_q[c // 2][:, (c % 2) * W : (c % 2 + 1) * W]
-            nc.vector.quantize_mx(codes.bitcast(FP8X4), o_s[:, cols], o_bf[c][:])
+        def plane_stage(c, codes):
+            half = codes[:, (c % 2) * W : (c % 2 + 1) * W]
+            nc.vector.quantize_mx(half.bitcast(FP8X4), out_scales[:, c * W : (c + 1) * W], out_bf[c][:])
 
+        fetch_stage(0)
+        fetch_stage(1)
         gate_stage(0)
-        cast_stage(0, nc.scalar.copy)
+        fetch_stage(2)
         gate_stage(1)
-        cast_stage(1, nc.scalar.copy)
+        fetch_stage(3)
+        round_stage(0, nc.scalar.copy)
+        round_stage(1, nc.scalar.copy)
         gate_stage(2)
-        cast_stage(2, nc.scalar.copy)
+        round_stage(2, nc.scalar.copy)
         gate_stage(3)
-        o_q = [tile([P, 2 * W], I32, "o_q0", "sig3"), tile([P, 2 * W], I32, "o_q1")]
-        plane_stage(0)
-        cast_stage(3, nc.vector.tensor_copy)
-        plane_stage(1)
-        nc.sync.dma_start(out_words[:, 0 : 2 * W], o_q[0][:])
-        plane_stage(2)
-        plane_stage(3)
-        nc.sync.dma_start(out_words[:, 2 * W : S], o_q[1][:])
-        for q in range(4):
-            eng = nc.scalar if q % 2 else nc.sync
-            eng.dma_start(out_2[0, 4 * q : 4 * q + 4, :].bitcast(I32), o_s[32 * q : 32 * q + 4, :].bitcast(I32))
+        codes_low = tile([P, 2 * W], I32, "codes_low", "gate_slot1")
+        codes_high = tile([P, 2 * W], I32, "codes_high")
+        plane_stage(0, codes_low)
+        round_stage(LAST, nc.vector.tensor_copy)
+        plane_stage(1, codes_low)
+        nc.sync.dma_start(words_of(out_1)[:, 0 : 2 * W], codes_low[:])
+        plane_stage(2, codes_high)
+        plane_stage(3, codes_high)
+        nc.sync.dma_start(words_of(out_1)[:, 2 * W : S], codes_high[:])
+        for q in range(QUADRANTS):
+            plane, rows = scale_rows(out_scales, out_2, q)
+            queue = nc.scalar if q % 2 else nc.sync
+            queue.dma_start(rows, plane)

from contextlib import ExitStack

import concourse.mybir as mybir

F32 = mybir.dt.float32
BF16 = mybir.dt.bfloat16
I32 = mybir.dt.int32
U32 = mybir.dt.uint32
U16 = mybir.dt.uint16
U8 = mybir.dt.uint8
FP8X4 = mybir.dt.float8_e4m3fn_x4
ALU = mybir.AluOpType
ACT = mybir.ActivationFunctionType

P = 128
PACK = 4
QUADRANTS = 4
T = 2048
S = 512
W = 128
CHUNKS = S // W
LAST = CHUNKS - 1
LIST_COLS = W // 16
LINE_BYTES = 16
SCALAR_ROWS = (0, 1)
VECTOR_ROWS = (3, 2)
FLOPS = 2 * 2 * S * S * S


def tile_picked_mixpick_none_po_kernel(
    tc, x_words, x_scales, wa, gt, w1_words, w1_scales, offs, fo, out_0, out_1, out_2
):
    nc = tc.nc
    with ExitStack() as ctx:
        sb = ctx.enter_context(tc.tile_pool(name="sb", bufs=1))
        ps = ctx.enter_context(tc.psum_pool(name="ps", bufs=1))

        def tile(shape, dtype, name, tag=""):
            return sb.tile(shape, dtype, name=name, tag=tag, align_bytes=64)

        def words_of(packed):
            return packed[0].rearrange("p n t -> p (n t)").bitcast(I32)

        def scale_rows(plane, rows, q):
            return plane[32 * q : 32 * q + 4, :].bitcast(I32), rows[0, 4 * q : 4 * q + 4, :].bitcast(I32)

        def deal(eng, dst, src, element_bytes):
            run = LINE_BYTES // element_bytes
            eng.tensor_copy(
                dst.rearrange("p (t c i) -> p c t i", t=PACK, i=run),
                src.rearrange("p (c i t) -> p c t i", t=PACK, i=run),
            )

        def interleaved(dst, src):
            run = LINE_BYTES // 4
            return (
                dst.rearrange("p (c i t) -> p c t i", i=run, t=PACK),
                src.rearrange("p t (c i) -> p c t i", i=run),
            )

        offs_t = sb.tile([P, S // 16], U16, name="offs_t")
        fo_t = sb.tile([P, S // 16], U16, name="fo_t")
        xs_win = tile([P, T], U8, "xs_win", "after_byte_gather")
        gt_t = tile([P, PACK], F32, "gt_t")
        warm = tile([P, 1], F32, "warm")
        warm_out = tile([P, 1], F32, "warm_out")
        w1s_raw = tile([P, S], U8, "w1s_raw")

        nc.gpsimd.memset(xs_win[:].bitcast(I32), 0)
        nc.gpsimd.memset(warm[:], 0.0)
        nc.gpsimd.memset(w1s_raw[:].bitcast(I32), 0)
        for q in range(QUADRANTS // 2):
            nc.gpsimd.dma_start(*scale_rows(w1s_raw, w1_scales, q))

        wa_rows = wa.rearrange("(p j) n -> p j n", j=PACK)
        wa_raw = {}

        def load_wa_half(half):
            raw = tile([P, PACK, 2 * W], F32, f"wa_raw{half}", f"after_wa_half{half}")
            nc.sync.dma_start(raw[:], wa_rows[:, :, 2 * half * W : 2 * (half + 1) * W])
            wa_raw[2 * half], wa_raw[2 * half + 1] = raw[:, :, 0:W], raw[:, :, W : 2 * W]

        nc.sync.dma_start(offs_t[:], offs)
        load_wa_half(0)
        for q in range(QUADRANTS):
            queue = nc.sync if q < QUADRANTS // 2 else nc.scalar
            queue.dma_start(*scale_rows(xs_win, x_scales, q))
        nc.scalar.activation(warm_out[:], warm[:], ACT.Sigmoid)
        xw_win = tile([P, T], I32, "xw_win", "after_word_gather")
        nc.sync.dma_start(xw_win[:], words_of(x_words))
        load_wa_half(1)
        nc.sync.dma_start(gt_t[:], gt.rearrange("(p t) o -> p (t o)", t=PACK))
        for q in range(QUADRANTS // 2, QUADRANTS):
            nc.sync.dma_start(*scale_rows(w1s_raw, w1_scales, q))
        w1w_raw = tile([P, S], I32, "w1w_raw")
        nc.sync.dma_start(w1w_raw[:], words_of(w1_words))
        nc.sync.dma_start(fo_t[:], fo)

        wa_bf = [tile([P, W * PACK], BF16, f"wa_bf{c}", f"after_wa_quant{c}") for c in range(CHUNKS)]
        for c in range(LAST):
            nc.scalar.copy(*interleaved(wa_bf[c][:], wa_raw[c]))

        def quantised(values, name, tag=""):
            codes = tile([P, W], U32, f"{name}_q", tag)
            scales = tile([P, W], U8, f"{name}_s")
            nc.vector.quantize_mx(codes[:].bitcast(FP8X4), scales[:], values)
            return codes[:], scales[:]

        xs_got = tile([P, S], U8, "xs_got", "after_byte_deal")
        xs = tile([P, S], U8, "xs")
        nc.vector.tensor_copy(xs_got[:], xs_win[:].indirect(offs_t[:]))
        deal(nc.vector, xs[:], xs_got[:], 1)
        wa_mx = {0: quantised(wa_bf[0][:], "wa0", "after_byte_gather"), 1: quantised(wa_bf[1][:], "wa1")}
        xw = tile([P, S], U32, "xw", "after_byte_deal")
        nc.vector.tensor_copy(xw[:].rearrange("p (t m) -> p m t", t=PACK), xw_win[:].bitcast(U32).indirect(offs_t[:]))

        w1s = tile([P, S], U8, "w1s", "after_word_gather")
        deal(nc.vector, w1s[:], w1s_raw[:], 1)
        nc.vector.tensor_copy(*interleaved(wa_bf[LAST][:], wa_raw[LAST]))
        wa_mx[3] = quantised(wa_bf[3][:], "wa3")
        wa_mx[2] = quantised(wa_bf[2][:], "wa2")
        w1w = tile([P, S], I32, "w1w", "after_wa_quant3")
        deal(nc.gpsimd, w1w[:], w1w_raw[:], 4)

        h_win = {t: tile([P, S], F32, f"h_win{t}") for t in SCALAR_ROWS}
        sig_win = {t: tile([P, S], F32, f"sig_win{t}") for t in VECTOR_ROWS}
        z_bf, h_banks = {}, {}

        def product(outs, lhs_words, lhs_scales, rhs):
            for t, out in outs.items():
                cols = slice(t * P, (t + 1) * P)
                nc.tensor.matmul_mx(
                    out=out,
                    lhsT=lhs_words[:, cols].bitcast(FP8X4),
                    lhsT_scale=lhs_scales[:, cols],
                    rhs=rhs[0].bitcast(FP8X4),
                    rhs_scale=rhs[1],
                    start=True,
                    stop=True,
                )

        def z_stage(c, tag=""):
            bank = ps.tile([P, PACK, W], F32, name=f"y_ps{c}", tag=f"y{c}")
            product({t: bank[:, t, :] for t in range(PACK)}, xw, xs, wa_mx[c])
            z_bf[c] = tile([P, W, PACK], BF16, f"z_bf{c}", tag)
            nc.vector.scalar_tensor_tensor(
                out=z_bf[c][:],
                in0=bank[:].rearrange("p t j -> p j t"),
                scalar=0.0,
                in1=gt_t[:].unsqueeze(1).to_broadcast([P, W, PACK]),
                op0=ALU.max,
                op1=ALU.mult,
            )

        def h_stage(c):
            z_mx = quantised(z_bf[c][:].rearrange("p j t -> p (j t)"), f"z{c}")
            cols = slice(c * W, (c + 1) * W)
            if c < LAST:
                h_banks[c] = [(0, PACK, ps.tile([P, PACK, W], F32, name=f"h_ps{c}"))]
                rows, copy = range(PACK), nc.scalar.copy
            else:
                h_banks[c] = [
                    (2, PACK, ps.tile([P, 2, W], F32, name="h_ps_upper")),
                    (0, 2, ps.tile([P, 2, W], F32, name="h_ps_lower", tag="y0")),
                ]
                rows, copy = VECTOR_ROWS + SCALAR_ROWS, nc.vector.tensor_copy
            h = {t: bank[:, t - a, :] for a, b, bank in h_banks[c] for t in range(a, b)}
            product({t: h[t] for t in rows}, w1w, w1s, z_mx)
            for t in VECTOR_ROWS:
                nc.scalar.activation(sig_win[t][:, cols], h[t], ACT.Sigmoid)
            for t in SCALAR_ROWS:
                copy(h_win[t][:, cols], h[t])

        z_stage(0, "after_wa_half1")
        z_stage(1, "after_wa_quant2")
        h_stage(0)
        z_stage(2)
        h_stage(1)
        z_stage(3)
        h_stage(2)
        h_stage(3)

        out_rows = out_0.rearrange("(p t) j -> p t j", t=PACK)
        out_scales = tile([P, S], U8, "out_scales")
        gate, out_f32, out_bf = {}, {}, {}

        def fetch_stage(c):
            picks = fo_t[:, c * LIST_COLS : (c + 1) * LIST_COLS]
            gate[c] = tile([P, PACK, W], F32, f"gate{c}", f"gate_slot{c % 2}")
            for t in SCALAR_ROWS:
                nc.scalar.activation(gate[c][:, t, :], h_win[t][:].indirect(picks), ACT.Sigmoid)
            for t in sorted(VECTOR_ROWS):
                nc.vector.tensor_copy(gate[c][:, t, :], sig_win[t][:].indirect(picks))

        def gate_stage(c):
            out_f32[c] = tile([P, PACK, W], F32, f"out_f32_{c}")
            for a, b, bank in h_banks[c]:
                nc.vector.tensor_tensor(out_f32[c][:, a:b, :], bank[:], gate[c][:, a:b, :], ALU.mult)
            nc.sync.dma_start(out_rows[:, :, c * W : (c + 1) * W], out_f32[c][:])

        def round_stage(c, copy):
            out_bf[c] = tile([P, W * PACK], BF16, f"out_bf{c}")
            copy(*interleaved(out_bf[c][:], out_f32[c][:]))

        def plane_stage(c, codes):
            half = codes[:, (c % 2) * W : (c % 2 + 1) * W]
            nc.vector.quantize_mx(half.bitcast(FP8X4), out_scales[:, c * W : (c + 1) * W], out_bf[c][:])

        fetch_stage(0)
        fetch_stage(1)
        gate_stage(0)
        fetch_stage(2)
        gate_stage(1)
        fetch_stage(3)
        round_stage(0, nc.scalar.copy)
        round_stage(1, nc.scalar.copy)
        gate_stage(2)
        round_stage(2, nc.scalar.copy)
        gate_stage(3)
        codes_low = tile([P, 2 * W], I32, "codes_low", "gate_slot1")
        codes_high = tile([P, 2 * W], I32, "codes_high")
        plane_stage(0, codes_low)
        round_stage(LAST, nc.vector.tensor_copy)
        plane_stage(1, codes_low)
        nc.sync.dma_start(words_of(out_1)[:, 0 : 2 * W], codes_low[:])
        plane_stage(2, codes_high)
        plane_stage(3, codes_high)
        nc.sync.dma_start(words_of(out_1)[:, 2 * W : S], codes_high[:])
        for q in range(QUADRANTS):
            plane, rows = scale_rows(out_scales, out_2, q)
            queue = nc.scalar if q % 2 else nc.sync
            queue.dma_start(rows, plane)
